import numpy as np
import ml_dtypes


def mxq(x, axis, fmt="e4m3"):
    dtype, down = {"e4m3": (ml_dtypes.float8_e4m3fn, 7), "e5m2": (ml_dtypes.float8_e5m2, 14)}[fmt]
    v = np.moveaxis(np.asarray(x, np.float32).astype(ml_dtypes.bfloat16).astype(np.float64), axis, -1)
    blocks = v.reshape(v.shape[:-1] + (-1, 32))
    amax = np.abs(blocks).max(-1, keepdims=True)
    byte = np.maximum(np.where(amax > 0, np.frexp(amax)[1] - 1 + 127, 0) - down, 1)
    scale = np.exp2(byte - 127.0)
    codes = (blocks / scale).astype(np.float32).astype(dtype).astype(np.float64)
    return np.moveaxis((codes * scale).reshape(v.shape), -1, axis)


WIDE = False


def mx_kscale(k):
    if not WIDE:
        return np.ones(k)
    levels = np.array([10, -10, 5, -5, 0])
    if k % 512:
        return np.exp2(np.random.permutation(np.resize(levels, k // 32))).repeat(32)
    a = np.empty((k // 512, 16))
    for p in range(k // 512):
        a[p, :8] = np.random.permutation(np.resize(levels, 8))
        for g in range(8):
            far = levels[np.abs(levels - a[p, g]) >= 10]
            a[p, g + 8] = far[np.random.randint(len(far))]
    return np.exp2(a.ravel()).repeat(32)


BF16 = ml_dtypes.bfloat16


def bf(x):
    return np.asarray(x, np.float32).astype(BF16)


def f64(x):
    return np.asarray(x).astype(np.float64)


E2M1 = np.array([0.0, 0.5, 1.0, 1.5, 2.0, 3.0, 4.0, 6.0, -0.0, -0.5, -1.0, -1.5, -2.0, -3.0, -4.0, -6.0])


def pack_weight(w, fmt):
    k, n = w.shape
    w = f64(bf(w)).reshape(k // 32, 32, n)
    amax = np.abs(w).max(1)
    if fmt == "e4m3":
        byte = np.frexp(amax)[1] - 1 + 127 - 7
    else:
        mant, ex = np.frexp(amax / 6.0)
        byte = np.where(mant > 0.5, ex, ex - 1) + 127
    byte = np.clip(np.where(amax > 0, byte, 1), 1, 254)
    scaled = (w * np.exp2(127.0 - byte)[:, None, :]).reshape(k, n).astype(np.float32)
    by_word = np.ascontiguousarray(scaled.reshape(k // 512, 128, 4, n).transpose(0, 1, 3, 2))
    if fmt == "e4m3":
        words = by_word.astype(ml_dtypes.float8_e4m3fn).view(np.uint8)
    else:
        c = by_word.astype(ml_dtypes.float4_e2m1fn).view(np.uint8) & 0xF
        words = c[..., 0::2] | (c[..., 1::2] << 4)
    return np.ascontiguousarray(words), np.ascontiguousarray(byte.astype(np.uint8).reshape(k // 512, 16, n))


def unpack_weight(words, scales, fmt):
    g, p, n, _ = words.shape
    if fmt == "e4m3":
        vals = np.ascontiguousarray(words).view(ml_dtypes.float8_e4m3fn).astype(np.float64)
    else:
        nib = np.empty((g, p, n, 4), np.uint8)
        nib[..., 0::2] = words & 0xF
        nib[..., 1::2] = words >> 4
        vals = E2M1[nib]
    vals = vals * np.repeat(np.exp2(scales.astype(np.float64) - 127.0), 8, axis=1)[..., None]
    return vals.transpose(0, 1, 3, 2).reshape(g * 512, n)
def pack4(w):
    words, scales = pack_weight(w, "e2m1")
    return words.reshape(words.shape[0], 128, -1), scales


def unpack4(words, scales):
    return unpack_weight(words.reshape(words.shape[0], 128, -1, 2), scales, "e2m1")


def planes(Y):
    n, m = Y.shape
    b = f64(bf(Y)).reshape(n // 32, 32, m)
    amax = np.abs(b).max(1)
    byte = np.clip(np.where(amax > 0, np.frexp(amax)[1] - 1 + 127 - 7, 1), 1, 254)
    codes = (b * np.exp2(127.0 - byte)[:, None, :]).reshape(n, m).astype(np.float32).astype(ml_dtypes.float8_e4m3fn).view(np.uint8)
    words = codes.reshape(n // 512, 128, 4, m).transpose(0, 1, 3, 2)
    return np.ascontiguousarray(words), np.ascontiguousarray(byte.astype(np.uint8).reshape(n // 512, 16, m))


L, S, P, E = 1024, 1024, 1536, 1536


def setup_inputs():
    s_state = mx_kscale(S)
    s_input = mx_kscale(P)
    spread = np.exp(0.8 * np.random.randn(E))
    H = np.random.randn(L, S)
    U = np.random.randn(L, P)
    C = 1.2 * np.random.randn(S, E) / np.sqrt(S) * spread[None, :]
    D = 1.0 * np.random.randn(P, E) / np.sqrt(P) * spread[None, :]
    Z = 1.5 * np.random.randn(L, E)
    D_words, D_scales = pack4(D / s_input[:, None])
    return {
        "H": bf(H * s_state[None, :]),
        "C": bf(C / s_state[:, None]),
        "U": bf(U * s_input[None, :]),
        "D_words": D_words,
        "D_scales": D_scales,
        "Z": bf(Z),
    }

def reference(H, C, U, D_words, D_scales, Z):
    h = mxq(f64(H), 1, "e4m3")
    c = mxq(f64(C), 0, "e4m3")
    readout = h @ c
    u = mxq(f64(U), 1, "e4m3")
    d = unpack4(D_words, D_scales)
    skip = u @ d
    z = f64(Z)
    gate = z / (1.0 + np.exp(-z))
    y = (readout + skip) * gate
    Y = y.T
    words, scales = planes(Y)
    return y, words, scales

@@ -1,0 +1,354 @@
+from contextlib import ExitStack
+
+import concourse.mybir as mybir
+from concourse.masks import make_identity
+
+L, S, PI, E = 1024, 1024, 1536, 1536
+FLOPS = 2 * L * (S + PI) * E
+
+F32 = mybir.dt.float32
+BF16 = mybir.dt.bfloat16
+I32 = mybir.dt.int32
+U32 = mybir.dt.uint32
+U8 = mybir.dt.uint8
+FP8X4 = mybir.dt.float8_e4m3fn_x4
+FP4X4 = mybir.dt.float4_e2m1fn_x4
+SILU = mybir.ActivationFunctionType.Silu
+MULT = mybir.AluOpType.mult
+
+P = 128
+KP = 512
+NT = 512
+TILES = L // P
+GROUPS = E // NT
+H_PASSES = S // KP
+U_PASSES = PI // KP
+UNITS = TILES * GROUPS
+BANKS = 4
+
+
+def tile_ssm_readout_silu_gate_g5_kernel(tc, H, C, U, D_words, D_scales, Z, out_0, out_1, out_2):
+    nc = tc.nc
+    with ExitStack() as ctx:
+        keep = ctx.enter_context(tc.tile_pool(name="keep", bufs=1))
+        ring = ctx.enter_context(tc.tile_pool(name="ring", bufs=1))
+        psum = ctx.enter_context(tc.psum_pool(name="psum", bufs=1))
+        ctx.enter_context(tc.manual_schedule())
+
+        ident = keep.tile([P, P], F32, name="ident")
+        d_scale = keep.tile([P, U_PASSES, E], U8, name="d_scale", align_bytes=64)
+        y_codes = [keep.tile([P, L], U32, name="y_codes%d" % g, align_bytes=64) for g in range(GROUPS)]
+        y_scale = [keep.tile([P, L], U8, name="y_scale%d" % g, align_bytes=64) for g in range(GROUPS)]
+
+        raw = {}
+        z_raw = {}
+        c_raw = {}
+        d_codes = {}
+        c_grouped = {}
+        c_operand = {}
+        act_operand = {}
+        acc = {}
+        gate = {}
+        y_pair = {}
+        y_half = {}
+        banks = {}
+        staged = {}
+        turns = []
+
+        def load_u(m):
+            t = keep.tile([P, PI], BF16, name="u_raw%d" % m)
+            nc.sync.dma_start(out=t[:], in_=U[m * P:(m + 1) * P, :])
+            raw[("u", m)] = t[:].bitcast(F32)
+
+        def load_h(m):
+            t = keep.tile([P, 2, S], BF16, name="h_raw%d" % m)
+            nc.sync.dma_start(out=t[:], in_=H[m * P:(m + 2) * P, :].rearrange("(t p) k -> p t k", p=P))
+            for i in range(2):
+                raw[("h", m + i)] = t[:, i, :].bitcast(F32)
+
+        def load_z(m0, m1, g0, g1):
+            t = keep.tile([P, m1 - m0, (g1 - g0) * NT], BF16, name="z_raw%d_%d" % (m0, g0))
+            nc.sync.dma_start(out=t[:], in_=Z[m0 * P:m1 * P, g0 * NT:g1 * NT].rearrange("(t p) n -> p t n", p=P))
+            for m in range(m0, m1):
+                for g in range(g0, g1):
+                    z_raw[g * TILES + m] = t[:, m - m0, (g - g0) * NT:(g - g0 + 1) * NT]
+
+        def load_c(g, c):
+            t = ring.tile([P, 4, NT], BF16, name="c_raw", tag="c_raw", bufs=4)
+            nc.sync.dma_start(out=t[:], in_=C[c * KP:(c + 1) * KP, g * NT:(g + 1) * NT].rearrange("(p j) n -> p j n", j=4))
+            c_raw[(g, c)] = t
+
+        def load_d(g0, g1):
+            t = keep.tile([P, U_PASSES, (g1 - g0) * 2 * NT], U8, name="d_codes%d" % g0, align_bytes=64)
+            src = D_words[:, :, g0 * 2 * NT:g1 * 2 * NT].rearrange("c p b -> p c b")
+            nc.sync.dma_start(out=t[:].bitcast(I32), in_=src.bitcast(I32))
+            for g in range(g0, g1):
+                for c in range(U_PASSES):
+                    d_codes[(g, c)] = t[:, c, (g - g0) * 2 * NT:(g - g0 + 1) * 2 * NT]
+
+        def load_d_scales():
+            for q in range(4):
+                src = D_scales[:, 4 * q:4 * q + 4, :].rearrange("c r n -> r c n")
+                nc.sync.dma_start(out=d_scale[32 * q:32 * q + 4, :, :].bitcast(I32), in_=src.bitcast(I32))
+
+        def interleave_c(g, c, part, parts, copy):
+            if part == 0:
+                c_grouped[(g, c)] = ring.tile([P, NT, 4], BF16, name="c_grouped", tag="c_grouped", bufs=2, align_bytes=64)
+            cols = slice(part * NT // parts, (part + 1) * NT // parts)
+            copy(
+                out=c_grouped[(g, c)][:, cols, :].rearrange("p (a i) t -> p a t i", i=4),
+                in_=c_raw[(g, c)][:, :, cols].rearrange("p t (a i) -> p a t i", i=4),
+            )
+
+        def quantize_c(g, c):
+            codes = keep.tile([P, NT], U32, name="c_codes%d_%d" % (g, c), align_bytes=64)
+            scale = keep.tile([P, NT], U8, name="c_scale%d_%d" % (g, c), align_bytes=64)
+            nc.vector.quantize_mx(
+                out=codes[:].bitcast(FP8X4), scales=scale[:], in_=c_grouped[(g, c)][:].rearrange("p n t -> p (n t)")
+            )
+            c_operand[(g, c)] = (codes, scale)
+
+        def turn(job, s):
+            if s == 0:
+                tag = "turn%d" % (len(turns) % BANKS)
+                turns.append(job)
+                banks[job] = psum.tile([P, 2, 2, P], F32, name=tag, tag=tag)
+            kind, m, c = job[s]
+            for u in range(2):
+                if kind == "y":
+                    words = y_half[c * TILES + m][:].bitcast(F32)[:, u * P:(u + 1) * P]
+                else:
+                    words = raw[(kind, m)][:, 2 * P * c + u:2 * P * (c + 1):2]
+                nc.tensor.transpose(banks[job][:, s, u, :], words, ident[:])
+
+        def turn_job(job):
+            turn(job, 0)
+            turn(job, 1)
+
+        def empty_bank(job):
+            t = ring.tile([P, 2 * KP], BF16, name="staged", tag="staged", bufs=6, align_bytes=64)
+            nc.scalar.copy(
+                out=t[:].bitcast(F32).rearrange("p (s r u) -> p s r u", s=2, u=2),
+                in_=banks[job][:].rearrange("p s u r -> p s r u"),
+            )
+            staged[job] = t
+
+        def quantize_act(job):
+            kind, m, c = job[0]
+            codes = keep.tile([P, 2 * P], U32, name="a_codes_%s%d_%d" % (kind, m, c), align_bytes=64)
+            scale = keep.tile([P, 2 * P], U8, name="a_scale_%s%d_%d" % (kind, m, c), align_bytes=64)
+            nc.vector.quantize_mx(out=codes[:].bitcast(FP8X4), scales=scale[:], in_=staged[job][:])
+            for s in range(2):
+                act_operand[job[s]] = (codes[:, s * P:(s + 1) * P], scale[:, s * P:(s + 1) * P])
+
+        def quantize_y(job):
+            kind, m, g = job[0]
+            cols = slice(m * P, (m + 2) * P)
+            nc.vector.quantize_mx(out=y_codes[g][:, cols].bitcast(FP8X4), scales=y_scale[g][:, cols], in_=staged[job][:])
+
+        def mx_pass(g, slot):
+            kind, m, c = slot
+            n = g * TILES + m
+            first = kind == "u" and c == 0
+            last = kind == "h" and c == H_PASSES - 1
+            if first:
+                tag = "acc%d" % (n % BANKS)
+                acc[n] = psum.tile([P, NT], F32, name=tag, tag=tag)
+            if kind == "u":
+                rhs = d_codes[(g, c)].bitcast(FP4X4)
+                rhs_scale = d_scale[:, c, g * NT:(g + 1) * NT]
+            else:
+                rhs = c_operand[(g, c)][0][:].bitcast(FP8X4)
+                rhs_scale = c_operand[(g, c)][1][:]
+            codes, scale = act_operand[slot]
+            nc.tensor.matmul_mx(
+                out=acc[n][:], lhsT=codes.bitcast(FP8X4), lhsT_scale=scale, rhs=rhs, rhs_scale=rhs_scale,
+                start=first, stop=last,
+            )
+
+        def unit_passes(n):
+            g, m = divmod(n, TILES)
+            for c in range(U_PASSES):
+                mx_pass(g, ("u", m, c))
+            for c in range(H_PASSES):
+                mx_pass(g, ("h", m, c))
+
+        def silu(n):
+            gate[n] = ring.tile([P, NT], F32, name="gate", tag="gate", bufs=6)
+            nc.scalar.activation(out=gate[n][:], in_=z_raw[n], func=SILU)
+
+        def store_y(n, count):
+            g, m = divmod(n, TILES)
+            nc.sync.dma_start(
+                out=out_0[m * P:(m + count) * P, g * NT:(g + 1) * NT].rearrange("(t p) n -> p t n", p=P),
+                in_=y_pair[n // 2][:, n % 2:n % 2 + count, :],
+            )
+
+        def apply_gate(n):
+            if n % 2 == 0:
+                y_pair[n // 2] = ring.tile([P, 2, NT], F32, name="y_pair", tag="y_pair", bufs=5)
+            nc.vector.tensor_tensor(out=y_pair[n // 2][:, n % 2, :], in0=acc[n][:], in1=gate[n][:], op=MULT)
+            if n >= UNITS - 2:
+                store_y(n, 1)
+            elif n % 2 == 1:
+                store_y(n - 1, 2)
+
+        def round_y(n):
+            y_half[n] = ring.tile([P, NT], BF16, name="y_half", tag="y_half", bufs=10)
+            nc.vector.tensor_copy(
+                out=y_half[n][:].rearrange("t (u p e) -> t u p e", u=2, e=2),
+                in_=y_pair[n // 2][:, n % 2, :].rearrange("t (p u e) -> t u p e", u=2, e=2),
+            )
+
+        def store_codes(g, m0, m1):
+            dst = out_1[g].rearrange("p m t -> p (m t)")[:, 4 * m0 * P:4 * m1 * P]
+            nc.sync.dma_start(out=dst.bitcast(I32), in_=y_codes[g][:, m0 * P:m1 * P].bitcast(I32))
+
+        def store_scales(g, queues):
+            for q in range(4):
+                queues[q].dma_start(
+                    out=out_2[g, 4 * q:4 * q + 4, :].bitcast(I32), in_=y_scale[g][32 * q:32 * q + 4, :].bitcast(I32)
+                )
+
+        def pairs(slots):
+            return [(slots[i], slots[i + 1]) for i in range(0, len(slots), 2)]
+
+        def slots_of(kind, m0, m1):
+            return [(kind, m, c) for m in range(m0, m1) for c in range(U_PASSES if kind == "u" else H_PASSES)]
+
+        jobs = []
+        for m0, m1 in ((0, 4), (4, 6), (6, 8)):
+            jobs.extend(pairs(slots_of("u", m0, m1)) + pairs(slots_of("h", m0, m1)))
+        runs = pairs(jobs)
+        y_jobs = pairs([("y", m, g) for g in range(GROUPS) for m in range(TILES)])
+
+        nc.vector.memset(d_scale[:].rearrange("p c n -> p (c n)").bitcast(I32), 0)
+        make_identity(nc, ident[:])
+        load_u(0)
+        load_z(0, 1, 0, 1)
+        load_u(1)
+        load_d_scales()
+        load_d(0, 1)
+        load_u(2)
+        load_u(3)
+        load_c(0, 0)
+        load_h(0)
+        load_c(0, 1)
+        load_h(2)
+        load_z(1, 4, 0, 1)
+        load_u(4)
+        load_u(5)
+        load_h(4)
+        load_z(4, 8, 0, 1)
+        load_u(6)
+        load_u(7)
+        load_h(6)
+        load_c(1, 0)
+        silu(0)
+
+        vcopy = nc.vector.tensor_copy
+        scopy = nc.scalar.copy
+
+        for r in range(len(runs)):
+            a, b = runs[r]
+            turn_job(a)
+            turn_job(b)
+            if r >= 1:
+                for job in runs[r - 1]:
+                    for slot in job:
+                        mx_pass(0, slot)
+            if r in (8, 9):
+                interleave_c(1, 1, 2 * (r - 8), 4, scopy)
+            empty_bank(a)
+            empty_bank(b)
+            if r in (8, 9):
+                interleave_c(1, 1, 2 * (r - 8) + 1, 4, scopy)
+            if r in (2, 3, 7):
+                g, c = {2: (0, 0), 3: (0, 1), 7: (1, 0)}[r]
+                interleave_c(g, c, 0, 2, vcopy)
+                quantize_act(a)
+                interleave_c(g, c, 1, 2, vcopy)
+                quantize_act(b)
+                quantize_c(g, c)
+            elif r in (5, 6):
+                apply_gate(2 * (r - 5))
+                apply_gate(2 * (r - 5) + 1)
+                if r == 5:
+                    load_c(1, 1)
+                else:
+                    load_d(1, 3)
+                    load_z(0, 2, 1, 3)
+                    load_z(2, 4, 1, 3)
+                    load_c(2, 1)
+                    load_c(2, 0)
+                    load_z(4, 6, 1, 3)
+                    load_z(6, 8, 1, 3)
+                quantize_act(a)
+                round_y(r - 5)
+                quantize_act(b)
+            elif r == 8:
+                apply_gate(4)
+                round_y(2)
+                quantize_act(a)
+                round_y(3)
+                quantize_act(b)
+            elif r == 9:
+                apply_gate(5)
+                round_y(4)
+                quantize_act(a)
+                quantize_act(b)
+            else:
+                quantize_act(a)
+                quantize_act(b)
+            for n in {3: (1,), 4: (2, 3), 5: (4,), 6: (5,), 7: (6, 7)}.get(r, ()):
+                silu(n)
+
+        for job in runs[-1]:
+            for slot in job:
+                mx_pass(0, slot)
+        quantize_c(1, 1)
+        round_y(5)
+        silu(8)
+        silu(9)
+        apply_gate(6)
+
+        out_runs = {9: y_jobs[0:4], 17: y_jobs[4:8], 21: y_jobs[8:10]}
+        for n in range(TILES, UNITS):
+            unit_passes(n)
+            apply_gate(n - 1)
+            round_y(n - 2)
+            for job in out_runs.get(n, ()):
+                turn_job(job)
+            for job in out_runs.get(n - 1, [])[0:2] + out_runs.get(n - 2, [])[2:4]:
+                empty_bank(job)
+            if n + 2 < UNITS:
+                silu(n + 2)
+            if n in (8, 9, 12, 13):
+                interleave_c(2, 1, (8, 9, 12, 13).index(n), 4, scopy)
+            for job in out_runs.get(n - 2, [])[0:2] + out_runs.get(n - 3, [])[2:4]:
+                quantize_y(job)
+            if n in (12, 20):
+                store_codes((n - 12) // 8, 0, TILES)
+                store_scales((n - 12) // 8, [nc.sync] * 4)
+            if n == 23:
+                store_codes(2, 0, 4)
+            if n in (13, 14):
+                interleave_c(2, 0, n - 13, 2, vcopy)
+            if n == 14:
+                quantize_c(2, 1)
+            if n == 15:
+                quantize_c(2, 0)
+
+        round_y(UNITS - 2)
+        turn_job(y_jobs[10])
+        turn(y_jobs[11], 0)
+        apply_gate(UNITS - 1)
+        empty_bank(y_jobs[10])
+        round_y(UNITS - 1)
+        turn(y_jobs[11], 1)
+        quantize_y(y_jobs[10])
+        store_codes(2, 4, 6)
+        empty_bank(y_jobs[11])
+        quantize_y(y_jobs[11])
+        store_codes(2, 6, 8)
+        store_scales(2, [nc.scalar, nc.sync, nc.scalar, nc.sync])

@@ -36,7 +36,13 @@ def tile_ssm_readout_silu_gate_g5_kernel(tc, H, C, U, D_words, D_scales, Z, out_
         ctx.enter_context(tc.manual_schedule())
 
         ident = keep.tile([P, P], F32, name="ident")
-        d_scale = keep.tile([P, U_PASSES, E], U8, name="d_scale", align_bytes=64)
+        d_planes = {}
+        d_scale = {}
+        for g0, g1 in ((0, 1), (1, 3)):
+            d_planes[g0] = keep.tile([P, U_PASSES, (g1 - g0) * NT], U8, name="d_scale%d" % g0, align_bytes=64)
+            for g in range(g0, g1):
+                for c in range(U_PASSES):
+                    d_scale[(g, c)] = d_planes[g0][:, c, (g - g0) * NT:(g - g0 + 1) * NT]
         y_codes = [keep.tile([P, L], U32, name="y_codes%d" % g, align_bytes=64) for g in range(GROUPS)]
         y_scale = [keep.tile([P, L], U8, name="y_scale%d" % g, align_bytes=64) for g in range(GROUPS)]
 
@@ -86,18 +92,18 @@ def tile_ssm_readout_silu_gate_g5_kernel(tc, H, C, U, D_words, D_scales, Z, out_
                 for c in range(U_PASSES):
                     d_codes[(g, c)] = t[:, c, (g - g0) * 2 * NT:(g - g0 + 1) * 2 * NT]
 
-        def load_d_scales():
+        def load_d_scales(g0, g1):
             for q in range(4):
-                src = D_scales[:, 4 * q:4 * q + 4, :].rearrange("c r n -> r c n")
-                nc.sync.dma_start(out=d_scale[32 * q:32 * q + 4, :, :].bitcast(I32), in_=src.bitcast(I32))
+                src = D_scales[:, 4 * q:4 * q + 4, g0 * NT:g1 * NT].rearrange("c r n -> r c n")
+                nc.sync.dma_start(out=d_planes[g0][32 * q:32 * q + 4, :, :].bitcast(I32), in_=src.bitcast(I32))
 
         def interleave_c(g, c, part, parts, copy):
             if part == 0:
                 c_grouped[(g, c)] = ring.tile([P, NT, 4], BF16, name="c_grouped", tag="c_grouped", bufs=2, align_bytes=64)
             cols = slice(part * NT // parts, (part + 1) * NT // parts)
             copy(
-                out=c_grouped[(g, c)][:, cols, :].rearrange("p (a i) t -> p a t i", i=4),
-                in_=c_raw[(g, c)][:, :, cols].rearrange("p t (a i) -> p a t i", i=4),
+                out=c_grouped[(g, c)][:, cols, :],
+                in_=c_raw[(g, c)][:, :, cols].rearrange("p t n -> p n t"),
             )
 
         def quantize_c(g, c):
@@ -108,43 +114,39 @@ def tile_ssm_readout_silu_gate_g5_kernel(tc, H, C, U, D_words, D_scales, Z, out_
             )
             c_operand[(g, c)] = (codes, scale)
 
-        def turn(job, s):
-            if s == 0:
-                tag = "turn%d" % (len(turns) % BANKS)
-                turns.append(job)
-                banks[job] = psum.tile([P, 2, 2, P], F32, name=tag, tag=tag)
-            kind, m, c = job[s]
-            for u in range(2):
-                if kind == "y":
-                    words = y_half[c * TILES + m][:].bitcast(F32)[:, u * P:(u + 1) * P]
-                else:
-                    words = raw[(kind, m)][:, 2 * P * c + u:2 * P * (c + 1):2]
-                nc.tensor.transpose(banks[job][:, s, u, :], words, ident[:])
-
         def turn_job(job):
-            turn(job, 0)
-            turn(job, 1)
+            tag = "turn%d" % (len(turns) % BANKS)
+            turns.append(job)
+            banks[job] = psum.tile([P, 2, 2, P], F32, name=tag, tag=tag)
+            for s in range(len(job)):
+                kind, m, c = job[s]
+                for u in range(2):
+                    if kind == "y":
+                        words = y_half[c * TILES + m][:].bitcast(F32)[:, u * P:(u + 1) * P]
+                    else:
+                        words = raw[(kind, m)][:, 2 * P * c + u:2 * P * (c + 1):2]
+                    nc.tensor.transpose(banks[job][:, s, u, :], words, ident[:])
 
-        def empty_bank(job):
+        def empty_bank(job, copy):
             t = ring.tile([P, 2 * KP], BF16, name="staged", tag="staged", bufs=6, align_bytes=64)
-            nc.scalar.copy(
-                out=t[:].bitcast(F32).rearrange("p (s r u) -> p s r u", s=2, u=2),
-                in_=banks[job][:].rearrange("p s u r -> p s r u"),
+            staged[job] = t[:, 0:len(job) * KP]
+            copy(
+                out=staged[job].bitcast(F32).rearrange("p (s r u) -> p s r u", s=len(job), u=2),
+                in_=banks[job][:, 0:len(job), :, :].rearrange("p s u r -> p s r u"),
             )
-            staged[job] = t
 
         def quantize_act(job):
             kind, m, c = job[0]
             codes = keep.tile([P, 2 * P], U32, name="a_codes_%s%d_%d" % (kind, m, c), align_bytes=64)
             scale = keep.tile([P, 2 * P], U8, name="a_scale_%s%d_%d" % (kind, m, c), align_bytes=64)
-            nc.vector.quantize_mx(out=codes[:].bitcast(FP8X4), scales=scale[:], in_=staged[job][:])
+            nc.vector.quantize_mx(out=codes[:].bitcast(FP8X4), scales=scale[:], in_=staged[job])
             for s in range(2):
                 act_operand[job[s]] = (codes[:, s * P:(s + 1) * P], scale[:, s * P:(s + 1) * P])
 
         def quantize_y(job):
             kind, m, g = job[0]
-            cols = slice(m * P, (m + 2) * P)
-            nc.vector.quantize_mx(out=y_codes[g][:, cols].bitcast(FP8X4), scales=y_scale[g][:, cols], in_=staged[job][:])
+            cols = slice(m * P, (m + len(job)) * P)
+            nc.vector.quantize_mx(out=y_codes[g][:, cols].bitcast(FP8X4), scales=y_scale[g][:, cols], in_=staged[job])
 
         def mx_pass(g, slot):
             kind, m, c = slot
@@ -156,7 +158,7 @@ def tile_ssm_readout_silu_gate_g5_kernel(tc, H, C, U, D_words, D_scales, Z, out_
                 acc[n] = psum.tile([P, NT], F32, name=tag, tag=tag)
             if kind == "u":
                 rhs = d_codes[(g, c)].bitcast(FP4X4)
-                rhs_scale = d_scale[:, c, g * NT:(g + 1) * NT]
+                rhs_scale = d_scale[(g, c)]
             else:
                 rhs = c_operand[(g, c)][0][:].bitcast(FP8X4)
                 rhs_scale = c_operand[(g, c)][1][:]
@@ -186,12 +188,21 @@ def tile_ssm_readout_silu_gate_g5_kernel(tc, H, C, U, D_words, D_scales, Z, out_
 
         def apply_gate(n):
             if n % 2 == 0:
-                y_pair[n // 2] = ring.tile([P, 2, NT], F32, name="y_pair", tag="y_pair", bufs=5)
+                y_pair[n // 2] = ring.tile([P, 2, NT], F32, name="y_pair", tag="y_pair", bufs=7)
             nc.vector.tensor_tensor(out=y_pair[n // 2][:, n % 2, :], in0=acc[n][:], in1=gate[n][:], op=MULT)
             if n >= UNITS - 2:
                 store_y(n, 1)
-            elif n % 2 == 1:
+            elif n % 2 == 1 and n > 5:
                 store_y(n - 1, 2)
+
+        def gate_and_round(n):
+            y_half[n] = ring.tile([P, NT], BF16, name="y_half", tag="y_half", bufs=10)
+            nc.vector.tensor_tensor(
+                out=y_half[n][:].rearrange("t (u p e) -> t u p e", u=2, e=2),
+                in0=acc[n][:].rearrange("t (p u e) -> t u p e", u=2, e=2),
+                in1=gate[n][:].rearrange("t (p u e) -> t u p e", u=2, e=2),
+                op=MULT,
+            )
 
         def round_y(n):
             y_half[n] = ring.tile([P, NT], BF16, name="y_half", tag="y_half", bufs=10)
@@ -222,28 +233,34 @@ def tile_ssm_readout_silu_gate_g5_kernel(tc, H, C, U, D_words, D_scales, Z, out_
         runs = pairs(jobs)
         y_jobs = pairs([("y", m, g) for g in range(GROUPS) for m in range(TILES)])
 
-        nc.vector.memset(d_scale[:].rearrange("p c n -> p (c n)").bitcast(I32), 0)
+        for g0 in (0, 1):
+            nc.vector.memset(d_planes[g0][:].rearrange("p c n -> p (c n)").bitcast(I32), 0)
         make_identity(nc, ident[:])
         load_u(0)
-        load_z(0, 1, 0, 1)
         load_u(1)
-        load_d_scales()
-        load_d(0, 1)
         load_u(2)
+        load_d_scales(0, 1)
+        load_d(0, 1)
+        load_z(0, 1, 0, 1)
         load_u(3)
         load_c(0, 0)
         load_h(0)
         load_c(0, 1)
         load_h(2)
-        load_z(1, 4, 0, 1)
         load_u(4)
         load_u(5)
+        load_z(1, 4, 0, 1)
         load_h(4)
-        load_z(4, 8, 0, 1)
         load_u(6)
-        load_u(7)
-        load_h(6)
         load_c(1, 0)
+        load_z(4, 8, 0, 1)
+        load_u(7)
+        load_c(1, 1)
+        load_h(6)
+        load_d(1, 3)
+        load_d_scales(1, 3)
+        load_z(0, 2, 1, 3)
+        load_z(2, 4, 1, 3)
         silu(0)
 
         vcopy = nc.vector.tensor_copy
@@ -259,8 +276,8 @@ def tile_ssm_readout_silu_gate_g5_kernel(tc, H, C, U, D_words, D_scales, Z, out_
                         mx_pass(0, slot)
             if r in (8, 9):
                 interleave_c(1, 1, 2 * (r - 8), 4, scopy)
-            empty_bank(a)
-            empty_bank(b)
+            empty_bank(a, vcopy if r < 2 else scopy)
+            empty_bank(b, vcopy if r < 2 else scopy)
             if r in (8, 9):
                 interleave_c(1, 1, 2 * (r - 8) + 1, 4, scopy)
             if r in (2, 3, 7):
@@ -273,16 +290,6 @@ def tile_ssm_readout_silu_gate_g5_kernel(tc, H, C, U, D_words, D_scales, Z, out_
             elif r in (5, 6):
                 apply_gate(2 * (r - 5))
                 apply_gate(2 * (r - 5) + 1)
-                if r == 5:
-                    load_c(1, 1)
-                else:
-                    load_d(1, 3)
-                    load_z(0, 2, 1, 3)
-                    load_z(2, 4, 1, 3)
-                    load_c(2, 1)
-                    load_c(2, 0)
-                    load_z(4, 6, 1, 3)
-                    load_z(6, 8, 1, 3)
                 quantize_act(a)
                 round_y(r - 5)
                 quantize_act(b)
@@ -300,55 +307,70 @@ def tile_ssm_readout_silu_gate_g5_kernel(tc, H, C, U, D_words, D_scales, Z, out_
             else:
                 quantize_act(a)
                 quantize_act(b)
-            for n in {3: (1,), 4: (2, 3), 5: (4,), 6: (5,), 7: (6, 7)}.get(r, ()):
+            for n in {4: (1,), 5: (2, 3), 6: (4,), 7: (5, 6)}.get(r, ()):
                 silu(n)
+
+        store_y(0, 2)
+        load_c(2, 0)
+        load_z(4, 6, 1, 3)
+        load_c(2, 1)
+        load_z(6, 8, 1, 3)
+        store_y(2, 2)
+        store_y(4, 2)
 
         for job in runs[-1]:
             for slot in job:
                 mx_pass(0, slot)
         quantize_c(1, 1)
         round_y(5)
+        silu(7)
         silu(8)
         silu(9)
         apply_gate(6)
 
-        out_runs = {9: y_jobs[0:4], 17: y_jobs[4:8], 21: y_jobs[8:10]}
-        for n in range(TILES, UNITS):
+        out_runs = {9: y_jobs[0:4], 17: y_jobs[4:8]}
+        for n in range(TILES, UNITS - 1):
             unit_passes(n)
             apply_gate(n - 1)
             round_y(n - 2)
             for job in out_runs.get(n, ()):
                 turn_job(job)
             for job in out_runs.get(n - 1, [])[0:2] + out_runs.get(n - 2, [])[2:4]:
-                empty_bank(job)
+                empty_bank(job, scopy)
             if n + 2 < UNITS:
                 silu(n + 2)
-            if n in (8, 9, 12, 13):
-                interleave_c(2, 1, (8, 9, 12, 13).index(n), 4, scopy)
+            for part in {12: (0, 1), 13: (2,), 14: (3,)}.get(n, ()):
+                interleave_c(2, 1, part, 4, scopy)
             for job in out_runs.get(n - 2, [])[0:2] + out_runs.get(n - 3, [])[2:4]:
                 quantize_y(job)
             if n in (12, 20):
                 store_codes((n - 12) // 8, 0, TILES)
                 store_scales((n - 12) // 8, [nc.sync] * 4)
-            if n == 23:
-                store_codes(2, 0, 4)
-            if n in (13, 14):
-                interleave_c(2, 0, n - 13, 2, vcopy)
-            if n == 14:
-                quantize_c(2, 1)
-            if n == 15:
-                quantize_c(2, 0)
+            if n in (10, 13):
+                interleave_c(2, 0, (n - 10) // 3, 2, vcopy)
+            if n in (14, 15):
+                quantize_c(2, n - 14)
 
+        round_y(UNITS - 3)
+        for job in y_jobs[8:11]:
+            turn_job(job)
+        unit_passes(UNITS - 1)
+        for job in y_jobs[8:11]:
+            empty_bank(job, scopy)
+        apply_gate(UNITS - 2)
+        quantize_y(y_jobs[8])
         round_y(UNITS - 2)
-        turn_job(y_jobs[10])
-        turn(y_jobs[11], 0)
-        apply_gate(UNITS - 1)
-        empty_bank(y_jobs[10])
-        round_y(UNITS - 1)
-        turn(y_jobs[11], 1)
+        quantize_y(y_jobs[9])
         quantize_y(y_jobs[10])
-        store_codes(2, 4, 6)
-        empty_bank(y_jobs[11])
-        quantize_y(y_jobs[11])
+        store_codes(2, 0, 6)
+        before_last, last = y_jobs[11][0:1], y_jobs[11][1:2]
+        turn_job(before_last)
+        empty_bank(before_last, scopy)
+        gate_and_round(UNITS - 1)
+        turn_job(last)
+        empty_bank(last, scopy)
+        quantize_y(before_last)
+        apply_gate(UNITS - 1)
+        quantize_y(last)
         store_codes(2, 6, 8)
         store_scales(2, [nc.scalar, nc.sync, nc.scalar, nc.sync])

@@ -25,6 +25,7 @@ H_PASSES = S // KP
 U_PASSES = PI // KP
 UNITS = TILES * GROUPS
 BANKS = 4
+SPLIT = 320
 
 
 def tile_ssm_readout_silu_gate_g5_kernel(tc, H, C, U, D_words, D_scales, Z, out_0, out_1, out_2):
@@ -77,7 +78,7 @@ def tile_ssm_readout_silu_gate_g5_kernel(tc, H, C, U, D_words, D_scales, Z, out_
             nc.sync.dma_start(out=t[:], in_=Z[m0 * P:m1 * P, g0 * NT:g1 * NT].rearrange("(t p) n -> p t n", p=P))
             for m in range(m0, m1):
                 for g in range(g0, g1):
-                    z_raw[g * TILES + m] = t[:, m - m0, (g - g0) * NT:(g - g0 + 1) * NT]
+                    z_raw[g * TILES + m] = (t, m - m0, slice((g - g0) * NT, (g - g0 + 1) * NT))
 
         def load_c(g, c):
             t = ring.tile([P, 4, NT], BF16, name="c_raw", tag="c_raw", bufs=4)
@@ -97,14 +98,10 @@ def tile_ssm_readout_silu_gate_g5_kernel(tc, H, C, U, D_words, D_scales, Z, out_
                 src = D_scales[:, 4 * q:4 * q + 4, g0 * NT:g1 * NT].rearrange("c r n -> r c n")
                 nc.sync.dma_start(out=d_planes[g0][32 * q:32 * q + 4, :, :].bitcast(I32), in_=src.bitcast(I32))
 
-        def interleave_c(g, c, part, parts, copy):
-            if part == 0:
+        def interleave_c(g, c, copy, cols):
+            if (g, c) not in c_grouped:
                 c_grouped[(g, c)] = ring.tile([P, NT, 4], BF16, name="c_grouped", tag="c_grouped", bufs=2, align_bytes=64)
-            cols = slice(part * NT // parts, (part + 1) * NT // parts)
-            copy(
-                out=c_grouped[(g, c)][:, cols, :],
-                in_=c_raw[(g, c)][:, :, cols].rearrange("p t n -> p n t"),
-            )
+            copy(out=c_grouped[(g, c)][:, cols, :], in_=c_raw[(g, c)][:, :, cols].rearrange("p t n -> p n t"))
 
         def quantize_c(g, c):
             codes = keep.tile([P, NT], U32, name="c_codes%d_%d" % (g, c), align_bytes=64)
@@ -122,31 +119,42 @@ def tile_ssm_readout_silu_gate_g5_kernel(tc, H, C, U, D_words, D_scales, Z, out_
                 kind, m, c = job[s]
                 for u in range(2):
                     if kind == "y":
-                        words = y_half[c * TILES + m][:].bitcast(F32)[:, u * P:(u + 1) * P]
+                        first = (2 * (m % 2) + u) * P
+                        words = y_half[(c * TILES + m) // 2][:].bitcast(F32)[:, first:first + P]
                     else:
                         words = raw[(kind, m)][:, 2 * P * c + u:2 * P * (c + 1):2]
                     nc.tensor.transpose(banks[job][:, s, u, :], words, ident[:])
 
-        def empty_bank(job, copy):
-            t = ring.tile([P, 2 * KP], BF16, name="staged", tag="staged", bufs=6, align_bytes=64)
-            staged[job] = t[:, 0:len(job) * KP]
-            copy(
-                out=staged[job].bitcast(F32).rearrange("p (s r u) -> p s r u", s=len(job), u=2),
-                in_=banks[job][:, 0:len(job), :, :].rearrange("p s u r -> p s r u"),
+        def empty_banks(run, copy):
+            t = ring.tile([P, 4 * KP], BF16, name="staged", tag="staged", bufs=4, align_bytes=64)
+            staged[run] = t
+            for i in range(len(run)):
+                job = run[i]
+                copy(
+                    out=t[:, 2 * i * KP:(2 * i + len(job)) * KP].bitcast(F32).rearrange("p (s r u) -> p s r u", s=len(job), u=2),
+                    in_=banks[job][:, 0:len(job), :, :].rearrange("p s u r -> p s r u"),
+                )
+
+        def quantize_act(run, widths):
+            slots = run[0] + run[1]
+            kind, m, c = slots[0]
+            codes = keep.tile([P, 4 * P], U32, name="a_codes_%s%d_%d" % (kind, m, c), align_bytes=64)
+            scale = keep.tile([P, 4 * P], U8, name="a_scale_%s%d_%d" % (kind, m, c), align_bytes=64)
+            for s in range(0, 4, widths):
+                cols = slice(s * P, (s + widths) * P)
+                nc.vector.quantize_mx(
+                    out=codes[:, cols].bitcast(FP8X4), scales=scale[:, cols], in_=staged[run][:, s * KP:(s + widths) * KP]
+                )
+            for s in range(4):
+                act_operand[slots[s]] = (codes[:, s * P:(s + 1) * P], scale[:, s * P:(s + 1) * P])
+
+        def quantize_y(run):
+            kind, m, g = run[0][0]
+            count = sum(len(job) for job in run)
+            cols = slice(m * P, (m + count) * P)
+            nc.vector.quantize_mx(
+                out=y_codes[g][:, cols].bitcast(FP8X4), scales=y_scale[g][:, cols], in_=staged[run][:, 0:count * KP]
             )
-
-        def quantize_act(job):
-            kind, m, c = job[0]
-            codes = keep.tile([P, 2 * P], U32, name="a_codes_%s%d_%d" % (kind, m, c), align_bytes=64)
-            scale = keep.tile([P, 2 * P], U8, name="a_scale_%s%d_%d" % (kind, m, c), align_bytes=64)
-            nc.vector.quantize_mx(out=codes[:].bitcast(FP8X4), scales=scale[:], in_=staged[job])
-            for s in range(2):
-                act_operand[job[s]] = (codes[:, s * P:(s + 1) * P], scale[:, s * P:(s + 1) * P])
-
-        def quantize_y(job):
-            kind, m, g = job[0]
-            cols = slice(m * P, (m + len(job)) * P)
-            nc.vector.quantize_mx(out=y_codes[g][:, cols].bitcast(FP8X4), scales=y_scale[g][:, cols], in_=staged[job])
 
         def mx_pass(g, slot):
             kind, m, c = slot
@@ -175,9 +183,11 @@ def tile_ssm_readout_silu_gate_g5_kernel(tc, H, C, U, D_words, D_scales, Z, out_
             for c in range(H_PASSES):
                 mx_pass(g, ("h", m, c))
 
-        def silu(n):
-            gate[n] = ring.tile([P, NT], F32, name="gate", tag="gate", bufs=6)
-            nc.scalar.activation(out=gate[n][:], in_=z_raw[n], func=SILU)
+        def silu(n, count):
+            if n % 2 == 0:
+                gate[n // 2] = ring.tile([P, 2, NT], F32, name="gate", tag="gate", bufs=4)
+            t, row, cols = z_raw[n]
+            nc.scalar.activation(out=gate[n // 2][:, n % 2:n % 2 + count, :], in_=t[:, row:row + count, cols], func=SILU)
 
         def store_y(n, count):
             g, m = divmod(n, TILES)
@@ -189,26 +199,27 @@ def tile_ssm_readout_silu_gate_g5_kernel(tc, H, C, U, D_words, D_scales, Z, out_
         def apply_gate(n):
             if n % 2 == 0:
                 y_pair[n // 2] = ring.tile([P, 2, NT], F32, name="y_pair", tag="y_pair", bufs=7)
-            nc.vector.tensor_tensor(out=y_pair[n // 2][:, n % 2, :], in0=acc[n][:], in1=gate[n][:], op=MULT)
+            nc.vector.tensor_tensor(out=y_pair[n // 2][:, n % 2, :], in0=acc[n][:], in1=gate[n // 2][:, n % 2, :], op=MULT)
             if n >= UNITS - 2:
                 store_y(n, 1)
             elif n % 2 == 1 and n > 5:
                 store_y(n - 1, 2)
 
         def gate_and_round(n):
-            y_half[n] = ring.tile([P, NT], BF16, name="y_half", tag="y_half", bufs=10)
             nc.vector.tensor_tensor(
-                out=y_half[n][:].rearrange("t (u p e) -> t u p e", u=2, e=2),
+                out=y_half[n // 2][:, n % 2 * NT:(n % 2 + 1) * NT].rearrange("t (u p e) -> t u p e", u=2, e=2),
                 in0=acc[n][:].rearrange("t (p u e) -> t u p e", u=2, e=2),
-                in1=gate[n][:].rearrange("t (p u e) -> t u p e", u=2, e=2),
+                in1=gate[n // 2][:, n % 2, :].rearrange("t (p u e) -> t u p e", u=2, e=2),
                 op=MULT,
             )
 
-        def round_y(n):
-            y_half[n] = ring.tile([P, NT], BF16, name="y_half", tag="y_half", bufs=10)
-            nc.vector.tensor_copy(
-                out=y_half[n][:].rearrange("t (u p e) -> t u p e", u=2, e=2),
-                in_=y_pair[n // 2][:, n % 2, :].rearrange("t (p u e) -> t u p e", u=2, e=2),
+        def round_y(n, count, copy):
+            if n % 2 == 0:
+                y_half[n // 2] = ring.tile([P, 2 * NT], BF16, name="y_half", tag="y_half", bufs=5)
+            rows = slice(n % 2, n % 2 + count)
+            copy(
+                out=y_half[n // 2][:, rows.start * NT:rows.stop * NT].rearrange("t (s u p e) -> t s u p e", s=count, u=2, e=2),
+                in_=y_pair[n // 2][:, rows, :].rearrange("t s (p u e) -> t s u p e", u=2, e=2),
             )
 
         def store_codes(g, m0, m1):
@@ -247,130 +258,129 @@ def tile_ssm_readout_silu_gate_g5_kernel(tc, H, C, U, D_words, D_scales, Z, out_
         load_h(0)
         load_c(0, 1)
         load_h(2)
+        load_z(1, 4, 0, 1)
         load_u(4)
         load_u(5)
-        load_z(1, 4, 0, 1)
         load_h(4)
         load_u(6)
-        load_c(1, 0)
         load_z(4, 8, 0, 1)
+        load_c(1, 0)
         load_u(7)
         load_c(1, 1)
         load_h(6)
-        load_d(1, 3)
+        load_d(1, 2)
         load_d_scales(1, 3)
         load_z(0, 2, 1, 3)
         load_z(2, 4, 1, 3)
-        silu(0)
+        silu(0, 1)
 
         vcopy = nc.vector.tensor_copy
         scopy = nc.scalar.copy
 
+        v_cols, s_cols = slice(0, SPLIT), slice(SPLIT, NT)
+        c_steps = {2: (0, 0), 3: (0, 1), 7: (1, 0), 8: (1, 1)}
+
+        def run_passes(run):
+            for slot in sorted(run[0] + run[1], key=lambda slot: slot[0] == "h" and slot[2]):
+                mx_pass(0, slot)
+
         for r in range(len(runs)):
-            a, b = runs[r]
-            turn_job(a)
-            turn_job(b)
+            run = runs[r]
+            for job in run:
+                turn_job(job)
+            if r - 1 in c_steps:
+                quantize_c(*c_steps[r - 1])
             if r >= 1:
-                for job in runs[r - 1]:
-                    for slot in job:
-                        mx_pass(0, slot)
-            if r in (8, 9):
-                interleave_c(1, 1, 2 * (r - 8), 4, scopy)
-            empty_bank(a, vcopy if r < 2 else scopy)
-            empty_bank(b, vcopy if r < 2 else scopy)
-            if r in (8, 9):
-                interleave_c(1, 1, 2 * (r - 8) + 1, 4, scopy)
-            if r in (2, 3, 7):
-                g, c = {2: (0, 0), 3: (0, 1), 7: (1, 0)}[r]
-                interleave_c(g, c, 0, 2, vcopy)
-                quantize_act(a)
-                interleave_c(g, c, 1, 2, vcopy)
-                quantize_act(b)
-                quantize_c(g, c)
-            elif r in (5, 6):
-                apply_gate(2 * (r - 5))
-                apply_gate(2 * (r - 5) + 1)
-                quantize_act(a)
-                round_y(r - 5)
-                quantize_act(b)
-            elif r == 8:
-                apply_gate(4)
-                round_y(2)
-                quantize_act(a)
-                round_y(3)
-                quantize_act(b)
-            elif r == 9:
+                run_passes(runs[r - 1])
+            if r == 6:
+                round_y(0, 2, vcopy)
+            for n in {5: (0, 1), 6: (2, 3), 8: (4,)}.get(r, ()):
+                apply_gate(n)
+            if r in c_steps and r != 8:
+                interleave_c(*c_steps[r], vcopy, v_cols)
+            empty_banks(run, vcopy if r < 2 else scopy)
+            if r in c_steps:
+                interleave_c(*c_steps[r], scopy, s_cols)
+            quantize_act(run, 2 if r == 0 else 4)
+            if r == 8:
+                interleave_c(*c_steps[r], vcopy, v_cols)
+            if r == 9:
                 apply_gate(5)
-                round_y(4)
-                quantize_act(a)
-                quantize_act(b)
-            else:
-                quantize_act(a)
-                quantize_act(b)
-            for n in {4: (1,), 5: (2, 3), 6: (4,), 7: (5, 6)}.get(r, ()):
-                silu(n)
+                round_y(2, 2, vcopy)
+            if r == 4:
+                silu(1, 1)
+            if r in (5, 6, 9):
+                silu({5: 2, 6: 4, 9: 6}[r], 2)
 
         store_y(0, 2)
         load_c(2, 0)
         load_z(4, 6, 1, 3)
         load_c(2, 1)
         load_z(6, 8, 1, 3)
+        load_d(2, 3)
         store_y(2, 2)
         store_y(4, 2)
 
-        for job in runs[-1]:
-            for slot in job:
-                mx_pass(0, slot)
-        quantize_c(1, 1)
-        round_y(5)
-        silu(7)
-        silu(8)
-        silu(9)
+        unit_passes(TILES)
+        run_passes(runs[-1])
+        round_y(4, 2, vcopy)
+        silu(8, 2)
+        silu(10, 2)
         apply_gate(6)
+        apply_gate(7)
 
-        out_runs = {9: y_jobs[0:4], 17: y_jobs[4:8]}
-        for n in range(TILES, UNITS - 1):
+        y_runs = pairs(y_jobs)
+        turn_after = {10: y_runs[0:2], 17: y_runs[2:4]}
+        for n in range(TILES + 1, UNITS - 1):
             unit_passes(n)
+            for run in turn_after.get(n - 2, [])[0:1]:
+                quantize_y(run)
             apply_gate(n - 1)
-            round_y(n - 2)
-            for job in out_runs.get(n, ()):
-                turn_job(job)
-            for job in out_runs.get(n - 1, [])[0:2] + out_runs.get(n - 2, [])[2:4]:
-                empty_bank(job, scopy)
-            if n + 2 < UNITS:
-                silu(n + 2)
-            for part in {12: (0, 1), 13: (2,), 14: (3,)}.get(n, ()):
-                interleave_c(2, 1, part, 4, scopy)
-            for job in out_runs.get(n - 2, [])[0:2] + out_runs.get(n - 3, [])[2:4]:
-                quantize_y(job)
-            if n in (12, 20):
-                store_codes((n - 12) // 8, 0, TILES)
-                store_scales((n - 12) // 8, [nc.sync] * 4)
-            if n in (10, 13):
-                interleave_c(2, 0, (n - 10) // 3, 2, vcopy)
-            if n in (14, 15):
-                quantize_c(2, n - 14)
+            for run in turn_after.get(n - 2, [])[1:2]:
+                quantize_y(run)
+            if n in (12, 19):
+                store_codes((n - 12) // 7, 0, TILES)
+                store_scales((n - 12) // 7, [nc.sync] * 4)
+            if n in (10, 14):
+                interleave_c(2, (n - 10) // 4, scopy, s_cols)
+                interleave_c(2, (n - 10) // 4, vcopy, v_cols)
+            if n in (11, 15):
+                quantize_c(2, (n - 11) // 4)
+            for first, copy in {9: [(6, vcopy)], 14: [(8, scopy)], 15: [(10, scopy)], 16: [(12, vcopy), (14, scopy)],
+                                18: [(16, vcopy)], 20: [(18, vcopy)]}.get(n, ()):
+                round_y(first, 2, copy)
+            for run in turn_after.get(n, ()):
+                for job in run:
+                    turn_job(job)
+            for run in turn_after.get(n - 1, ()):
+                empty_banks(run, scopy)
+            if n % 2 == 0 and n + 2 < UNITS:
+                silu(n + 2, 2)
 
-        round_y(UNITS - 3)
-        for job in y_jobs[8:11]:
-            turn_job(job)
-        unit_passes(UNITS - 1)
-        for job in y_jobs[8:11]:
-            empty_bank(job, scopy)
-        apply_gate(UNITS - 2)
-        quantize_y(y_jobs[8])
-        round_y(UNITS - 2)
-        quantize_y(y_jobs[9])
-        quantize_y(y_jobs[10])
-        store_codes(2, 0, 6)
-        before_last, last = y_jobs[11][0:1], y_jobs[11][1:2]
-        turn_job(before_last)
-        empty_bank(before_last, scopy)
-        gate_and_round(UNITS - 1)
-        turn_job(last)
-        empty_bank(last, scopy)
+        n = UNITS - 1
+        round_y(n - 3, 1, vcopy)
+        round_y(n - 2, 1, vcopy)
+        late = [y_runs[4], (y_jobs[10],)]
+        for run in late:
+            for job in run:
+                turn_job(job)
+        unit_passes(n)
+        apply_gate(n - 1)
+        round_y(n - 1, 1, vcopy)
+        for run in late:
+            empty_banks(run, scopy)
+        quantize_y(late[0])
+        store_codes(2, 0, 4)
+        before_last, last = (y_jobs[11][0:1],), (y_jobs[11][1:2],)
+        turn_job(before_last[0])
+        empty_banks(before_last, scopy)
+        gate_and_round(n)
+        apply_gate(n)
+        turn_job(last[0])
+        empty_banks(last, scopy)
+        quantize_y(late[1])
+        store_codes(2, 4, 6)
         quantize_y(before_last)
-        apply_gate(UNITS - 1)
         quantize_y(last)
         store_codes(2, 6, 8)
         store_scales(2, [nc.scalar, nc.sync, nc.scalar, nc.sync])

from contextlib import ExitStack

import concourse.mybir as mybir
from concourse.masks import make_identity

L, S, PI, E = 1024, 1024, 1536, 1536
FLOPS = 2 * L * (S + PI) * E

F32 = mybir.dt.float32
BF16 = mybir.dt.bfloat16
I32 = mybir.dt.int32
U32 = mybir.dt.uint32
U8 = mybir.dt.uint8
FP8X4 = mybir.dt.float8_e4m3fn_x4
FP4X4 = mybir.dt.float4_e2m1fn_x4
SILU = mybir.ActivationFunctionType.Silu
MULT = mybir.AluOpType.mult

P = 128
KP = 512
NT = 512
TILES = L // P
GROUPS = E // NT
H_PASSES = S // KP
U_PASSES = PI // KP
UNITS = TILES * GROUPS
BANKS = 4
SPLIT = 320


def tile_ssm_readout_silu_gate_g5_kernel(tc, H, C, U, D_words, D_scales, Z, out_0, out_1, out_2):
    nc = tc.nc
    with ExitStack() as ctx:
        keep = ctx.enter_context(tc.tile_pool(name="keep", bufs=1))
        ring = ctx.enter_context(tc.tile_pool(name="ring", bufs=1))
        psum = ctx.enter_context(tc.psum_pool(name="psum", bufs=1))
        ctx.enter_context(tc.manual_schedule())

        ident = keep.tile([P, P], F32, name="ident")
        d_planes = {}
        d_scale = {}
        for g0, g1 in ((0, 1), (1, 3)):
            d_planes[g0] = keep.tile([P, U_PASSES, (g1 - g0) * NT], U8, name="d_scale%d" % g0, align_bytes=64)
            for g in range(g0, g1):
                for c in range(U_PASSES):
                    d_scale[(g, c)] = d_planes[g0][:, c, (g - g0) * NT:(g - g0 + 1) * NT]
        y_codes = [keep.tile([P, L], U32, name="y_codes%d" % g, align_bytes=64) for g in range(GROUPS)]
        y_scale = [keep.tile([P, L], U8, name="y_scale%d" % g, align_bytes=64) for g in range(GROUPS)]

        raw = {}
        z_raw = {}
        c_raw = {}
        d_codes = {}
        c_grouped = {}
        c_operand = {}
        act_operand = {}
        acc = {}
        gate = {}
        y_pair = {}
        y_half = {}
        banks = {}
        staged = {}
        turns = []

        def load_u(m):
            t = keep.tile([P, PI], BF16, name="u_raw%d" % m)
            nc.sync.dma_start(out=t[:], in_=U[m * P:(m + 1) * P, :])
            raw[("u", m)] = t[:].bitcast(F32)

        def load_h(m):
            t = keep.tile([P, 2, S], BF16, name="h_raw%d" % m)
            nc.sync.dma_start(out=t[:], in_=H[m * P:(m + 2) * P, :].rearrange("(t p) k -> p t k", p=P))
            for i in range(2):
                raw[("h", m + i)] = t[:, i, :].bitcast(F32)

        def load_z(m0, m1, g0, g1):
            t = keep.tile([P, m1 - m0, (g1 - g0) * NT], BF16, name="z_raw%d_%d" % (m0, g0))
            nc.sync.dma_start(out=t[:], in_=Z[m0 * P:m1 * P, g0 * NT:g1 * NT].rearrange("(t p) n -> p t n", p=P))
            for m in range(m0, m1):
                for g in range(g0, g1):
                    z_raw[g * TILES + m] = (t, m - m0, slice((g - g0) * NT, (g - g0 + 1) * NT))

        def load_c(g, c):
            t = ring.tile([P, 4, NT], BF16, name="c_raw", tag="c_raw", bufs=4)
            nc.sync.dma_start(out=t[:], in_=C[c * KP:(c + 1) * KP, g * NT:(g + 1) * NT].rearrange("(p j) n -> p j n", j=4))
            c_raw[(g, c)] = t

        def load_d(g0, g1):
            t = keep.tile([P, U_PASSES, (g1 - g0) * 2 * NT], U8, name="d_codes%d" % g0, align_bytes=64)
            src = D_words[:, :, g0 * 2 * NT:g1 * 2 * NT].rearrange("c p b -> p c b")
            nc.sync.dma_start(out=t[:].bitcast(I32), in_=src.bitcast(I32))
            for g in range(g0, g1):
                for c in range(U_PASSES):
                    d_codes[(g, c)] = t[:, c, (g - g0) * 2 * NT:(g - g0 + 1) * 2 * NT]

        def load_d_scales(g0, g1):
            for q in range(4):
                src = D_scales[:, 4 * q:4 * q + 4, g0 * NT:g1 * NT].rearrange("c r n -> r c n")
                nc.sync.dma_start(out=d_planes[g0][32 * q:32 * q + 4, :, :].bitcast(I32), in_=src.bitcast(I32))

        def interleave_c(g, c, copy, cols):
            if (g, c) not in c_grouped:
                c_grouped[(g, c)] = ring.tile([P, NT, 4], BF16, name="c_grouped", tag="c_grouped", bufs=2, align_bytes=64)
            copy(out=c_grouped[(g, c)][:, cols, :], in_=c_raw[(g, c)][:, :, cols].rearrange("p t n -> p n t"))

        def quantize_c(g, c):
            codes = keep.tile([P, NT], U32, name="c_codes%d_%d" % (g, c), align_bytes=64)
            scale = keep.tile([P, NT], U8, name="c_scale%d_%d" % (g, c), align_bytes=64)
            nc.vector.quantize_mx(
                out=codes[:].bitcast(FP8X4), scales=scale[:], in_=c_grouped[(g, c)][:].rearrange("p n t -> p (n t)")
            )
            c_operand[(g, c)] = (codes, scale)

        def turn_job(job):
            tag = "turn%d" % (len(turns) % BANKS)
            turns.append(job)
            banks[job] = psum.tile([P, 2, 2, P], F32, name=tag, tag=tag)
            for s in range(len(job)):
                kind, m, c = job[s]
                for u in range(2):
                    if kind == "y":
                        first = (2 * (m % 2) + u) * P
                        words = y_half[(c * TILES + m) // 2][:].bitcast(F32)[:, first:first + P]
                    else:
                        words = raw[(kind, m)][:, 2 * P * c + u:2 * P * (c + 1):2]
                    nc.tensor.transpose(banks[job][:, s, u, :], words, ident[:])

        def empty_banks(run, copy):
            t = ring.tile([P, 4 * KP], BF16, name="staged", tag="staged", bufs=4, align_bytes=64)
            staged[run] = t
            for i in range(len(run)):
                job = run[i]
                copy(
                    out=t[:, 2 * i * KP:(2 * i + len(job)) * KP].bitcast(F32).rearrange("p (s r u) -> p s r u", s=len(job), u=2),
                    in_=banks[job][:, 0:len(job), :, :].rearrange("p s u r -> p s r u"),
                )

        def quantize_act(run, widths):
            slots = run[0] + run[1]
            kind, m, c = slots[0]
            codes = keep.tile([P, 4 * P], U32, name="a_codes_%s%d_%d" % (kind, m, c), align_bytes=64)
            scale = keep.tile([P, 4 * P], U8, name="a_scale_%s%d_%d" % (kind, m, c), align_bytes=64)
            for s in range(0, 4, widths):
                cols = slice(s * P, (s + widths) * P)
                nc.vector.quantize_mx(
                    out=codes[:, cols].bitcast(FP8X4), scales=scale[:, cols], in_=staged[run][:, s * KP:(s + widths) * KP]
                )
            for s in range(4):
                act_operand[slots[s]] = (codes[:, s * P:(s + 1) * P], scale[:, s * P:(s + 1) * P])

        def quantize_y(run):
            kind, m, g = run[0][0]
            count = sum(len(job) for job in run)
            cols = slice(m * P, (m + count) * P)
            nc.vector.quantize_mx(
                out=y_codes[g][:, cols].bitcast(FP8X4), scales=y_scale[g][:, cols], in_=staged[run][:, 0:count * KP]
            )

        def mx_pass(g, slot):
            kind, m, c = slot
            n = g * TILES + m
            first = kind == "u" and c == 0
            last = kind == "h" and c == H_PASSES - 1
            if first:
                tag = "acc%d" % (n % BANKS)
                acc[n] = psum.tile([P, NT], F32, name=tag, tag=tag)
            if kind == "u":
                rhs = d_codes[(g, c)].bitcast(FP4X4)
                rhs_scale = d_scale[(g, c)]
            else:
                rhs = c_operand[(g, c)][0][:].bitcast(FP8X4)
                rhs_scale = c_operand[(g, c)][1][:]
            codes, scale = act_operand[slot]
            nc.tensor.matmul_mx(
                out=acc[n][:], lhsT=codes.bitcast(FP8X4), lhsT_scale=scale, rhs=rhs, rhs_scale=rhs_scale,
                start=first, stop=last,
            )

        def unit_passes(n):
            g, m = divmod(n, TILES)
            for c in range(U_PASSES):
                mx_pass(g, ("u", m, c))
            for c in range(H_PASSES):
                mx_pass(g, ("h", m, c))

        def silu(n, count):
            if n % 2 == 0:
                gate[n // 2] = ring.tile([P, 2, NT], F32, name="gate", tag="gate", bufs=4)
            t, row, cols = z_raw[n]
            nc.scalar.activation(out=gate[n // 2][:, n % 2:n % 2 + count, :], in_=t[:, row:row + count, cols], func=SILU)

        def store_y(n, count):
            g, m = divmod(n, TILES)
            nc.sync.dma_start(
                out=out_0[m * P:(m + count) * P, g * NT:(g + 1) * NT].rearrange("(t p) n -> p t n", p=P),
                in_=y_pair[n // 2][:, n % 2:n % 2 + count, :],
            )

        def apply_gate(n):
            if n % 2 == 0:
                y_pair[n // 2] = ring.tile([P, 2, NT], F32, name="y_pair", tag="y_pair", bufs=7)
            nc.vector.tensor_tensor(out=y_pair[n // 2][:, n % 2, :], in0=acc[n][:], in1=gate[n // 2][:, n % 2, :], op=MULT)
            if n >= UNITS - 2:
                store_y(n, 1)
            elif n % 2 == 1 and n > 5:
                store_y(n - 1, 2)

        def gate_and_round(n):
            nc.vector.tensor_tensor(
                out=y_half[n // 2][:, n % 2 * NT:(n % 2 + 1) * NT].rearrange("t (u p e) -> t u p e", u=2, e=2),
                in0=acc[n][:].rearrange("t (p u e) -> t u p e", u=2, e=2),
                in1=gate[n // 2][:, n % 2, :].rearrange("t (p u e) -> t u p e", u=2, e=2),
                op=MULT,
            )

        def round_y(n, count, copy):
            if n % 2 == 0:
                y_half[n // 2] = ring.tile([P, 2 * NT], BF16, name="y_half", tag="y_half", bufs=5)
            rows = slice(n % 2, n % 2 + count)
            copy(
                out=y_half[n // 2][:, rows.start * NT:rows.stop * NT].rearrange("t (s u p e) -> t s u p e", s=count, u=2, e=2),
                in_=y_pair[n // 2][:, rows, :].rearrange("t s (p u e) -> t s u p e", u=2, e=2),
            )

        def store_codes(g, m0, m1):
            dst = out_1[g].rearrange("p m t -> p (m t)")[:, 4 * m0 * P:4 * m1 * P]
            nc.sync.dma_start(out=dst.bitcast(I32), in_=y_codes[g][:, m0 * P:m1 * P].bitcast(I32))

        def store_scales(g, queues):
            for q in range(4):
                queues[q].dma_start(
                    out=out_2[g, 4 * q:4 * q + 4, :].bitcast(I32), in_=y_scale[g][32 * q:32 * q + 4, :].bitcast(I32)
                )

        def pairs(slots):
            return [(slots[i], slots[i + 1]) for i in range(0, len(slots), 2)]

        def slots_of(kind, m0, m1):
            return [(kind, m, c) for m in range(m0, m1) for c in range(U_PASSES if kind == "u" else H_PASSES)]

        jobs = []
        for m0, m1 in ((0, 4), (4, 6), (6, 8)):
            jobs.extend(pairs(slots_of("u", m0, m1)) + pairs(slots_of("h", m0, m1)))
        runs = pairs(jobs)
        y_jobs = pairs([("y", m, g) for g in range(GROUPS) for m in range(TILES)])

        for g0 in (0, 1):
            nc.vector.memset(d_planes[g0][:].rearrange("p c n -> p (c n)").bitcast(I32), 0)
        make_identity(nc, ident[:])
        load_u(0)
        load_u(1)
        load_u(2)
        load_d_scales(0, 1)
        load_d(0, 1)
        load_z(0, 1, 0, 1)
        load_u(3)
        load_c(0, 0)
        load_h(0)
        load_c(0, 1)
        load_h(2)
        load_z(1, 4, 0, 1)
        load_u(4)
        load_u(5)
        load_h(4)
        load_u(6)
        load_z(4, 8, 0, 1)
        load_c(1, 0)
        load_u(7)
        load_c(1, 1)
        load_h(6)
        load_d(1, 2)
        load_d_scales(1, 3)
        load_z(0, 2, 1, 3)
        load_z(2, 4, 1, 3)
        silu(0, 1)

        vcopy = nc.vector.tensor_copy
        scopy = nc.scalar.copy

        v_cols, s_cols = slice(0, SPLIT), slice(SPLIT, NT)
        c_steps = {2: (0, 0), 3: (0, 1), 7: (1, 0), 8: (1, 1)}

        def run_passes(run):
            for slot in sorted(run[0] + run[1], key=lambda slot: slot[0] == "h" and slot[2]):
                mx_pass(0, slot)

        for r in range(len(runs)):
            run = runs[r]
            for job in run:
                turn_job(job)
            if r - 1 in c_steps:
                quantize_c(*c_steps[r - 1])
            if r >= 1:
                run_passes(runs[r - 1])
            if r == 6:
                round_y(0, 2, vcopy)
            for n in {5: (0, 1), 6: (2, 3), 8: (4,)}.get(r, ()):
                apply_gate(n)
            if r in c_steps and r != 8:
                interleave_c(*c_steps[r], vcopy, v_cols)
            empty_banks(run, vcopy if r < 2 else scopy)
            if r in c_steps:
                interleave_c(*c_steps[r], scopy, s_cols)
            quantize_act(run, 2 if r == 0 else 4)
            if r == 8:
                interleave_c(*c_steps[r], vcopy, v_cols)
            if r == 9:
                apply_gate(5)
                round_y(2, 2, vcopy)
            if r == 4:
                silu(1, 1)
            if r in (5, 6, 9):
                silu({5: 2, 6: 4, 9: 6}[r], 2)

        store_y(0, 2)
        load_c(2, 0)
        load_z(4, 6, 1, 3)
        load_c(2, 1)
        load_z(6, 8, 1, 3)
        load_d(2, 3)
        store_y(2, 2)
        store_y(4, 2)

        unit_passes(TILES)
        run_passes(runs[-1])
        round_y(4, 2, vcopy)
        silu(8, 2)
        silu(10, 2)
        apply_gate(6)
        apply_gate(7)

        y_runs = pairs(y_jobs)
        turn_after = {10: y_runs[0:2], 17: y_runs[2:4]}
        for n in range(TILES + 1, UNITS - 1):
            unit_passes(n)
            for run in turn_after.get(n - 2, [])[0:1]:
                quantize_y(run)
            apply_gate(n - 1)
            for run in turn_after.get(n - 2, [])[1:2]:
                quantize_y(run)
            if n in (12, 19):
                store_codes((n - 12) // 7, 0, TILES)
                store_scales((n - 12) // 7, [nc.sync] * 4)
            if n in (10, 14):
                interleave_c(2, (n - 10) // 4, scopy, s_cols)
                interleave_c(2, (n - 10) // 4, vcopy, v_cols)
            if n in (11, 15):
                quantize_c(2, (n - 11) // 4)
            for first, copy in {9: [(6, vcopy)], 14: [(8, scopy)], 15: [(10, scopy)], 16: [(12, vcopy), (14, scopy)],
                                18: [(16, vcopy)], 20: [(18, vcopy)]}.get(n, ()):
                round_y(first, 2, copy)
            for run in turn_after.get(n, ()):
                for job in run:
                    turn_job(job)
            for run in turn_after.get(n - 1, ()):
                empty_banks(run, scopy)
            if n % 2 == 0 and n + 2 < UNITS:
                silu(n + 2, 2)

        n = UNITS - 1
        round_y(n - 3, 1, vcopy)
        round_y(n - 2, 1, vcopy)
        late = [y_runs[4], (y_jobs[10],)]
        for run in late:
            for job in run:
                turn_job(job)
        unit_passes(n)
        apply_gate(n - 1)
        round_y(n - 1, 1, vcopy)
        for run in late:
            empty_banks(run, scopy)
        quantize_y(late[0])
        store_codes(2, 0, 4)
        before_last, last = (y_jobs[11][0:1],), (y_jobs[11][1:2],)
        turn_job(before_last[0])
        empty_banks(before_last, scopy)
        gate_and_round(n)
        apply_gate(n)
        turn_job(last[0])
        empty_banks(last, scopy)
        quantize_y(late[1])
        store_codes(2, 4, 6)
        quantize_y(before_last)
        quantize_y(last)
        store_codes(2, 6, 8)
        store_scales(2, [nc.scalar, nc.sync, nc.scalar, nc.sync])
